import numpy as np
import ml_dtypes


def mxq(x, axis, fmt="e4m3"):
    dtype, down = {"e4m3": (ml_dtypes.float8_e4m3fn, 7), "e5m2": (ml_dtypes.float8_e5m2, 14)}[fmt]
    v = np.moveaxis(np.asarray(x, np.float32).astype(ml_dtypes.bfloat16).astype(np.float64), axis, -1)
    blocks = v.reshape(v.shape[:-1] + (-1, 32))
    amax = np.abs(blocks).max(-1, keepdims=True)
    byte = np.maximum(np.where(amax > 0, np.frexp(amax)[1] - 1 + 127, 0) - down, 1)
    scale = np.exp2(byte - 127.0)
    codes = (blocks / scale).astype(np.float32).astype(dtype).astype(np.float64)
    return np.moveaxis((codes * scale).reshape(v.shape), -1, axis)


WIDE = False


def mx_kscale(k):
    if not WIDE:
        return np.ones(k)
    levels = np.array([10, -10, 5, -5, 0])
    if k % 512:
        return np.exp2(np.random.permutation(np.resize(levels, k // 32))).repeat(32)
    a = np.empty((k // 512, 16))
    for p in range(k // 512):
        a[p, :8] = np.random.permutation(np.resize(levels, 8))
        for g in range(8):
            far = levels[np.abs(levels - a[p, g]) >= 10]
            a[p, g + 8] = far[np.random.randint(len(far))]
    return np.exp2(a.ravel()).repeat(32)


def f64(x):
    return np.asarray(x).astype(np.float64)


def striped(idx):
    return np.tile(idx.reshape(-1, 16).T, (8, 1)).astype(np.uint16)


def unstriped(offs):
    return offs[:16].T.reshape(-1).astype(np.int64)


def striped8(idx):
    return np.concatenate([x.reshape(-1, 16).T for x in idx]).astype(np.uint16)


def runs(offs, k):
    lists = np.stack([offs[16 * r : 16 * r + 16].T.reshape(-1) for r in range(8)]).astype(np.int64)
    return lists[np.arange(k) % 512 // 64]


def pack_weight(w):
    k, n = w.shape
    w = f64(np.asarray(w, np.float32).astype(ml_dtypes.bfloat16)).reshape(k // 32, 32, n)
    amax = np.abs(w).max(1)
    byte = np.clip(np.where(amax > 0, np.frexp(amax)[1] - 1 + 127 - 7, 1), 1, 254)
    scaled = (w * np.exp2(127.0 - byte)[:, None, :]).reshape(k, n).astype(np.float32)
    words = np.ascontiguousarray(scaled.reshape(k // 512, 128, 4, n).transpose(0, 1, 3, 2)).astype(ml_dtypes.float8_e4m3fn).view(np.uint8)
    return words, np.ascontiguousarray(byte.astype(np.uint8).reshape(k // 512, 16, n))


def unpack_weight(words, scales):
    g, p, n, _ = words.shape
    vals = np.ascontiguousarray(words).view(ml_dtypes.float8_e4m3fn).astype(np.float64) * np.repeat(np.exp2(scales.astype(np.float64) - 127.0), 8, axis=1)[..., None]
    return vals.transpose(0, 1, 3, 2).reshape(g * 512, n)


def sigmoid(v):
    return 1.0 / (1.0 + np.exp(-np.maximum(v, -700.0)))

def planes(y):
    n, m = y.shape
    v = y.astype(np.float32).astype(ml_dtypes.bfloat16).astype(np.float64).reshape(n // 32, 32, m)
    top = np.abs(v).max(1)
    byte = np.clip(np.where(top > 0, np.frexp(top)[1] - 1 + 127 - 7, 1), 1, 254)
    codes = (v * np.exp2(127.0 - byte)[:, None, :]).reshape(n, m).astype(np.float32).astype(ml_dtypes.float8_e4m3fn).view(np.uint8)
    words = codes.reshape(n // 512, 128, 4, m).transpose(0, 1, 3, 2)
    return np.ascontiguousarray(words), np.ascontiguousarray(byte.astype(np.uint8).reshape(n // 512, 16, m))


K, T, S, N, H = 512, 2048, 512, 512, 512


def setup_inputs():
    n = np.random.standard_normal
    s = mx_kscale(K)[:, None]
    u = mx_kscale(H)
    packed_xT = pack_weight(n((K, T)) * s)
    packed_w1 = pack_weight(n((K, H)) / np.sqrt(K) / s)
    packed_w2 = pack_weight(n((K, H)) / np.sqrt(K) / s)
    packed_w3 = pack_weight(n((H, N)) / np.sqrt(H) / u[:, None])
    return {
        "x_words": packed_xT[0],
        "x_scales": packed_xT[1],
        "w1_words": packed_w1[0],
        "w1_scales": packed_w1[1],
        "w2_words": packed_w2[0],
        "w2_scales": packed_w2[1],
        "sl": np.random.uniform(1.0, 2.0, (H, 1)).astype(np.float32),
        "th": (0.5 * n((H, 1))).astype(np.float32),
        "gn": (np.random.uniform(0.5, 1.5, (H, 1)) * u[:, None]).astype(np.float32),
        "w3_words": packed_w3[0],
        "w3_scales": packed_w3[1],
        "tau": np.random.uniform(0.3, 0.9, (N, 1)).astype(np.float32),
        "offs": striped(np.random.permutation(T)[:S]),
        "hz": striped8(np.random.randint(0, T, (8, S))),
        "n1": striped(np.random.permutation(S)),
        "n2": striped(np.random.permutation(S)),
        "n3": striped8(np.stack([np.random.permutation(S) for _ in range(8)])),
        "n4": striped8(np.stack([np.random.permutation(S) for _ in range(8)])),
    }


def reference(x_words, x_scales, w1_words, w1_scales, w2_words, w2_scales, sl, th, gn, w3_words, w3_scales, tau, offs, hz, n1, n2, n3, n4):
    xq = unpack_weight(x_words, x_scales)[:, unstriped(offs)]
    y = unpack_weight(w1_words, w1_scales).T @ xq
    x_hz = unpack_weight(x_words, x_scales)[np.arange(K)[:, None], runs(hz, K)]
    d = unpack_weight(w2_words, w2_scales).T @ x_hz
    sg = sigmoid(f64(sl) * (d[:, unstriped(n1)] - f64(th)))
    z = f64(gn) * (y * sg - (0.5 * y[:, unstriped(n2)]))
    h = unpack_weight(w3_words, w3_scales).T @ mxq(z, 0, "e4m3")
    top = h.max(axis=1, keepdims=True)
    ea = np.exp(f64(tau) * (h[np.arange(N)[:, None], runs(n3, N)] - top))
    ea2 = np.exp(f64(tau) * (h[np.arange(N)[:, None], runs(n4, N)] - top))
    out_0 = h + np.log(ea + ea2 + 0.25)
    return (out_0,) + planes(out_0)

@@ -1,0 +1,263 @@
+from contextlib import ExitStack
+
+import concourse.mybir as mybir
+
+K, T, S, N, H = 512, 2048, 512, 512, 512
+FLOPS = 2 * K * H * S * 2 + 2 * H * N * S
+
+F32 = mybir.dt.float32
+BF16 = mybir.dt.bfloat16
+I32 = mybir.dt.int32
+U32 = mybir.dt.uint32
+U16 = mybir.dt.uint16
+U8 = mybir.dt.uint8
+FP8X4 = mybir.dt.float8_e4m3fn_x4
+ALU = mybir.AluOpType
+ACT = mybir.ActivationFunctionType
+
+P = 128
+PACK = 4
+LANES = 16
+BANK_COLS = 128
+HALF = S // 2
+Z_CHUNKS = ((0, (256,)), (HALF, (128, 128)))
+NEAR_ON_SCALAR = 0
+
+
+def words_of(dram):
+    return dram[0].rearrange("p n t -> p (n t)").bitcast(I32)
+
+
+def entries(offsets, first, count):
+    return offsets[:, first // LANES : (first + count) // LANES]
+
+
+def tile_picked_twhgxbelg_none_po_kernel(
+    tc, x_words, x_scales, w1_words, w1_scales, w2_words, w2_scales, sl, th, gn,
+    w3_words, w3_scales, tau, offs, hz, n1, n2, n3, n4, out_0, out_1, out_2,
+):
+    nc = tc.nc
+    with ExitStack() as ctx:
+        keep = ctx.enter_context(tc.tile_pool(name="keep", bufs=1))
+        psum = ctx.enter_context(tc.psum_pool(name="psum", bufs=1))
+
+        def sb(name, shape, dtype):
+            return keep.tile(shape, dtype, name=name, align_bytes=64)
+
+        def load_list(name, dram):
+            tile = sb(name, [P, S // LANES], U16)
+            nc.sync.dma_start(tile[:], dram)
+            return tile
+
+        def load_rows(queue, name, dram):
+            tile = sb(name, [P, PACK], F32)
+            queue.dma_start(tile[:], dram.rearrange("(p t) o -> p (t o)", t=PACK))
+            return tile
+
+        def load_scale_rows(queue, tile, first, dram):
+            rows = dram[0].bitcast(I32).rearrange("(q i) c -> i q c", i=4)
+            for i in range(4):
+                queue.dma_start(tile[first + i : P : 32, :].bitcast(I32), rows[i])
+
+        def deal(engine_copy, name, raw, dtype):
+            dealt = sb(name, [P, H], dtype)
+            engine_copy(
+                dealt[:].rearrange("p (t g i) -> p g t i", t=PACK, i=4),
+                raw[:].rearrange("p (g i t) -> p g t i", t=PACK, i=4),
+            )
+            return dealt
+
+        def interleaved(tile, width):
+            return tile.rearrange("p (c i t) -> p c t i", i=2, t=PACK)
+
+        def paired(tile):
+            return tile.rearrange("p t (c i) -> p c t i", i=2)
+
+        xs_table = sb("xs_table", [P, T], U8)
+        raw_planes = [sb(f"w{i}s_raw", [P, H], U8) for i in (1, 2, 3)]
+        nc.gpsimd.memset(xs_table[:].bitcast(I32), 0)
+        for tile in raw_planes:
+            nc.vector.memset(tile[:].bitcast(I32), 0)
+        warm_in = sb("warm_in", [P, 1], F32)
+        nc.vector.memset(warm_in[:], 0.0)
+        warm_out = sb("warm_out", [P, 1], F32)
+        nc.scalar.activation(warm_out[:], warm_in[:], ACT.Sigmoid)
+
+        def load_words(name, dram, width):
+            tile = sb(name, [P, width], U32)
+            nc.sync.dma_start(tile[:].bitcast(I32), words_of(dram))
+            return tile
+
+        hz_sb = load_list("hz_sb", hz)
+        xs_rows = x_scales[0].bitcast(I32)
+        by_run = xs_rows.rearrange("(r e) c -> e r c", e=2)
+        by_quad = xs_rows.rearrange("(q i) c -> i q c", i=4)
+        for e in range(2):
+            nc.sync.dma_start(xs_table[e:P:LANES, :].bitcast(I32), by_run[e])
+        for i in (2, 3):
+            nc.sync.dma_start(xs_table[i:P:32, :].bitcast(I32), by_quad[i])
+        offs_sb = load_list("offs_sb", offs)
+        xw_table = load_words("xw_table", x_words, T)
+        load_scale_rows(nc.sync, raw_planes[0], 0, w1_scales)
+        w1w_raw = load_words("w1w_raw", w1_words, H)
+        gn_sb = load_rows(nc.gpsimd, "gn_sb", gn)
+        w2w_raw = load_words("w2w_raw", w2_words, H)
+        load_scale_rows(nc.sync, raw_planes[1], 0, w2_scales)
+
+        hz_bytes = sb("hz_bytes", [P, S], U8)
+        nc.vector.tensor_copy(hz_bytes[:], xs_table[:].indirect(hz_sb[:]))
+        hz_plane = sb("hz_plane", [P, S], U8)
+        nc.vector.tensor_copy(hz_plane[:].bitcast(I32), hz_bytes[:].bitcast(I32))
+        for e in range(2):
+            nc.sync.dma_start(hz_plane[2 + e : P : 32, :].bitcast(I32), hz_bytes[LANES + e : P : 32, :].bitcast(I32))
+
+        sl_sb = load_rows(nc.gpsimd, "sl_sb", sl)
+        th_sb = load_rows(nc.gpsimd, "th_sb", th)
+        n2_sb = load_list("n2_sb", n2)
+        n1_sb = load_list("n1_sb", n1)
+        w3w_raw = load_words("w3w_raw", w3_words, N)
+        load_scale_rows(nc.sync, raw_planes[2], 0, w3_scales)
+        tau_sb = load_rows(nc.sync, "tau_sb", tau)
+        n3_sb = load_list("n3_sb", n3)
+        n4_sb = load_list("n4_sb", n4)
+
+        offs_plane = sb("offs_plane", [P, S], U8)
+        nc.vector.tensor_copy(offs_plane[:], xs_table[:].indirect(offs_sb[:]))
+        offs_words = sb("offs_words", [P, S], U32)
+        nc.vector.tensor_copy(offs_words[:], xw_table[:].indirect(offs_sb[:]))
+        hz_words = sb("hz_words", [P, S], U32)
+        nc.vector.tensor_copy(hz_words[:], xw_table[:].indirect(hz_sb[:]))
+
+        w1w = deal(nc.scalar.copy, "w1w", w1w_raw, U32)
+        w2w = deal(nc.scalar.copy, "w2w", w2w_raw, U32)
+        w1s = deal(nc.gpsimd.tensor_copy, "w1s", raw_planes[0], U8)
+        w2s = deal(nc.gpsimd.tensor_copy, "w2s", raw_planes[1], U8)
+        w3w = deal(nc.gpsimd.tensor_copy, "w3w", w3w_raw, U32)
+        w3s = deal(nc.gpsimd.tensor_copy, "w3s", raw_planes[2], U8)
+
+        half_gn = sb("half_gn", [P, PACK], F32)
+        nc.gpsimd.tensor_scalar(half_gn[:], gn_sb[:], -0.5, 0.0, ALU.mult, ALU.add)
+        minus_sl = sb("minus_sl", [P, PACK], F32)
+        nc.gpsimd.tensor_scalar(minus_sl[:], sl_sb[:], -1.0, 0.0, ALU.mult, ALU.add)
+        sg_bias = sb("sg_bias", [P, PACK], F32)
+        nc.gpsimd.tensor_tensor(sg_bias[:], minus_sl[:], th_sb[:], ALU.mult)
+
+        d_ps = [psum.tile([P, S], F32, name=f"d_ps{t}", tag=f"bank{t}") for t in range(PACK)]
+        y_ps = [psum.tile([P, S], F32, name=f"y_ps{t}", tag=f"bank{PACK + t}") for t in range(PACK)]
+
+        def product(out, w, w_plane, t, x, x_plane):
+            cols = slice(t * P, (t + 1) * P)
+            nc.tensor.matmul_mx(
+                out=out, lhsT=w[:, cols].bitcast(FP8X4), lhsT_scale=w_plane[:, cols],
+                rhs=x.bitcast(FP8X4), rhs_scale=x_plane, start=True, stop=True,
+            )
+
+        for t in range(PACK):
+            product(y_ps[t][:], w1w, w1s, t, offs_words[:], offs_plane[:])
+        for t in range(PACK):
+            product(d_ps[t][:], w2w, w2s, t, hz_words[:], hz_plane[:])
+
+        d_sb = [sb(f"d_sb{t}", [P, S], F32) for t in range(PACK)]
+        y_sb = [sb(f"y_sb{t}", [P, S], F32) for t in range(PACK)]
+        h_sg = [sb(f"h_sg{t}", [P, 2 * S], F32) for t in range(PACK)]
+        near = sb("near", [P, PACK, S], F32)
+        gated = sb("gated", [P, PACK, S], F32)
+        z_bf = sb("z_bf", [P, PACK * S], BF16)
+        z_words = sb("z_words", [P, S], U32)
+        z_plane = sb("z_plane", [P, S], U8)
+        tops = sb("tops", [P, PACK, PACK], F32)
+        ea_bias = sb("ea_bias", [P, PACK], F32)
+        h_ps = []
+
+        def h_out(t, c):
+            nc.vector.tensor_scalar(
+                h_sg[t][:, c * BANK_COLS : (c + 1) * BANK_COLS], h_ps[c][:, t, :], 1.0,
+                tops[:, t, c - 1 : c] if c else None, ALU.mult, ALU.max, accum_out=tops[:, t, c : c + 1],
+            )
+
+        for t in range(PACK):
+            nc.scalar.activation(y_sb[t][:], y_ps[t][:], ACT.Copy, scale=half_gn[:, t : t + 1])
+        def fetch_near(t, first, on_scalar):
+            window = y_sb[t][:].indirect(entries(n2_sb, first, HALF))
+            if on_scalar:
+                nc.scalar.activation(near[:, t, first : first + HALF], window, ACT.Copy)
+            else:
+                nc.vector.tensor_copy(near[:, t, first : first + HALF], window)
+
+        for t in range(PACK):
+            fetch_near(t, 0, False)
+        for t in range(PACK - NEAR_ON_SCALAR):
+            fetch_near(t, HALF, False)
+
+        for first, z_chunks in Z_CHUNKS:
+            half = slice(first, first + HALF)
+            for t in range(PACK):
+                if first == 0:
+                    nc.scalar.copy(d_sb[t][:], d_ps[t][:])
+                sg = h_sg[t][:, S + first : S + first + HALF]
+                nc.scalar.activation(
+                    sg, d_sb[t][:].indirect(entries(n1_sb, first, HALF)), ACT.Sigmoid,
+                    bias=sg_bias[:, t : t + 1], scale=sl_sb[:, t : t + 1],
+                )
+                nc.vector.scalar_tensor_tensor(
+                    gated[:, t, half], y_ps[t][:, half], gn_sb[:, t : t + 1], sg, ALU.mult, ALU.mult
+                )
+            if first:
+                for t in range(PACK - NEAR_ON_SCALAR, PACK):
+                    fetch_near(t, HALF, True)
+            for count in z_chunks:
+                cols = slice(first, first + count)
+                z_cols = z_bf[:, PACK * first : PACK * (first + count)]
+                nc.vector.tensor_tensor(interleaved(z_cols, count), paired(gated[:, :, cols]), paired(near[:, :, cols]), ALU.add)
+                nc.vector.quantize_mx(out=z_words[:, cols].bitcast(FP8X4), scales=z_plane[:, cols], in_=z_cols)
+                for c in range(first // BANK_COLS, (first + count) // BANK_COLS):
+                    bank = psum.tile([P, PACK, BANK_COLS], F32, name=f"h_ps{c}", tag=f"bank{c}")
+                    h_ps.append(bank)
+                    c_cols = slice(c * BANK_COLS, (c + 1) * BANK_COLS)
+                    for t in range(PACK):
+                        product(bank[:, t, :], w3w, w3s, t, z_words[:, c_cols], z_plane[:, c_cols])
+                    h_out(0, c)
+                first = first + count
+
+        total = sb("total", [P, PACK, S], F32)
+        for t in range(PACK):
+            if t:
+                for c in range(PACK):
+                    h_out(t, c)
+            nc.vector.scalar_tensor_tensor(
+                ea_bias[:, t : t + 1], tops[:, t, PACK - 1 : PACK], -1.0, tau_sb[:, t : t + 1], ALU.mult, ALU.mult
+            )
+            both = []
+            for name, lst in (("ea", n3_sb), ("eb", n4_sb)):
+                e = sb(f"{name}{t}", [P, S], F32)
+                nc.scalar.activation(
+                    e[:], h_sg[t][:].indirect(lst[:]), ACT.Exp, bias=ea_bias[:, t : t + 1], scale=tau_sb[:, t : t + 1]
+                )
+                both.append(e)
+            nc.vector.scalar_tensor_tensor(total[:, t, :], both[0][:], 0.25, both[1][:], ALU.add, ALU.add)
+
+        out_rows = out_0.rearrange("(p t) c -> p t c", t=PACK)
+        o_words = sb("o_words", [P, S], U32)
+        o_plane = sb("o_plane", [P, S], U8)
+        results = []
+        for c in range(PACK):
+            cols = slice(c * BANK_COLS, (c + 1) * BANK_COLS)
+            logs = sb(f"logs{c}", [P, PACK, BANK_COLS], F32)
+            nc.scalar.activation(logs[:], total[:, :, cols], ACT.Ln)
+            res = sb(f"res{c}", [P, PACK, BANK_COLS], F32)
+            nc.vector.tensor_tensor(res[:], logs[:], h_ps[c][:], ALU.add)
+            nc.sync.dma_start(out_rows[:, :, cols], res[:])
+            results.append(res)
+        round_copies = (nc.scalar.copy, nc.scalar.copy, nc.vector.tensor_copy, nc.vector.tensor_copy)
+        for c in range(PACK):
+            cols = slice(c * BANK_COLS, (c + 1) * BANK_COLS)
+            res_bf = sb(f"res_bf{c}", [P, PACK * BANK_COLS], BF16)
+            round_copies[c](interleaved(res_bf[:], BANK_COLS), paired(results[c][:]))
+            nc.vector.quantize_mx(out=o_words[:, cols].bitcast(FP8X4), scales=o_plane[:, cols], in_=res_bf[:])
+            if c % 2:
+                pair = slice((c - 1) * BANK_COLS, (c + 1) * BANK_COLS)
+                nc.sync.dma_start(words_of(out_1)[:, pair], o_words[:, pair].bitcast(I32))
+        plane_rows = out_2[0].bitcast(I32).rearrange("(q i) c -> i q c", i=4)
+        for i in range(4):
+            queue = nc.scalar if i % 2 else nc.sync
+            queue.dma_start(plane_rows[i], o_plane[i:P:32, :].bitcast(I32))

@@ -78,10 +78,6 @@ def tile_picked_twhgxbelg_none_po_kernel(
         nc.gpsimd.memset(xs_table[:].bitcast(I32), 0)
         for tile in raw_planes:
             nc.vector.memset(tile[:].bitcast(I32), 0)
-        warm_in = sb("warm_in", [P, 1], F32)
-        nc.vector.memset(warm_in[:], 0.0)
-        warm_out = sb("warm_out", [P, 1], F32)
-        nc.scalar.activation(warm_out[:], warm_in[:], ACT.Sigmoid)
 
         def load_words(name, dram, width):
             tile = sb(name, [P, width], U32)

@@ -20,8 +20,6 @@ PACK = 4
 LANES = 16
 BANK_COLS = 128
 HALF = S // 2
-Z_CHUNKS = ((0, (256,)), (HALF, (128, 128)))
-NEAR_ON_SCALAR = 0
 
 
 def words_of(dram):
@@ -41,8 +39,8 @@ def tile_picked_twhgxbelg_none_po_kernel(
         keep = ctx.enter_context(tc.tile_pool(name="keep", bufs=1))
         psum = ctx.enter_context(tc.psum_pool(name="psum", bufs=1))
 
-        def sb(name, shape, dtype):
-            return keep.tile(shape, dtype, name=name, align_bytes=64)
+        def sb(name, shape, dtype, tag=None):
+            return keep.tile(shape, dtype, name=name, tag=tag or name, align_bytes=64)
 
         def load_list(name, dram):
             tile = sb(name, [P, S // LANES], U16)
@@ -59,11 +57,12 @@ def tile_picked_twhgxbelg_none_po_kernel(
             for i in range(4):
                 queue.dma_start(tile[first + i : P : 32, :].bitcast(I32), rows[i])
 
-        def deal(engine_copy, name, raw, dtype):
-            dealt = sb(name, [P, H], dtype)
+        def deal(engine_copy, name, raw, dtype, tag=None):
+            dealt = sb(name, [P, H], dtype, tag=tag)
+            run = 16 if dtype == U8 else 4
             engine_copy(
-                dealt[:].rearrange("p (t g i) -> p g t i", t=PACK, i=4),
-                raw[:].rearrange("p (g i t) -> p g t i", t=PACK, i=4),
+                dealt[:].rearrange("p (t g i) -> p g t i", t=PACK, i=run),
+                raw[:].rearrange("p (g i t) -> p g t i", t=PACK, i=run),
             )
             return dealt
 
@@ -75,15 +74,19 @@ def tile_picked_twhgxbelg_none_po_kernel(
 
         xs_table = sb("xs_table", [P, T], U8)
         raw_planes = [sb(f"w{i}s_raw", [P, H], U8) for i in (1, 2, 3)]
-        nc.gpsimd.memset(xs_table[:].bitcast(I32), 0)
-        for tile in raw_planes:
+        for tile in [xs_table] + raw_planes:
             nc.vector.memset(tile[:].bitcast(I32), 0)
+        warm_in = sb("warm_in", [P, 1], F32)
+        nc.vector.memset(warm_in[:], 0.0)
+        warm_out = sb("warm_out", [P, 1], F32)
+        nc.scalar.activation(warm_out[:], warm_in[:], ACT.Sigmoid)
 
         def load_words(name, dram, width):
             tile = sb(name, [P, width], U32)
             nc.sync.dma_start(tile[:].bitcast(I32), words_of(dram))
             return tile
 
+        w1w_raw = load_words("w1w_raw", w1_words, H)
         hz_sb = load_list("hz_sb", hz)
         xs_rows = x_scales[0].bitcast(I32)
         by_run = xs_rows.rearrange("(r e) c -> e r c", e=2)
@@ -95,9 +98,10 @@ def tile_picked_twhgxbelg_none_po_kernel(
         offs_sb = load_list("offs_sb", offs)
         xw_table = load_words("xw_table", x_words, T)
         load_scale_rows(nc.sync, raw_planes[0], 0, w1_scales)
-        w1w_raw = load_words("w1w_raw", w1_words, H)
+        w3w_raw = load_words("w3w_raw", w3_words, N)
         gn_sb = load_rows(nc.gpsimd, "gn_sb", gn)
         w2w_raw = load_words("w2w_raw", w2_words, H)
+        n2_sb = load_list("n2_sb", n2)
         load_scale_rows(nc.sync, raw_planes[1], 0, w2_scales)
 
         hz_bytes = sb("hz_bytes", [P, S], U8)
@@ -107,11 +111,9 @@ def tile_picked_twhgxbelg_none_po_kernel(
         for e in range(2):
             nc.sync.dma_start(hz_plane[2 + e : P : 32, :].bitcast(I32), hz_bytes[LANES + e : P : 32, :].bitcast(I32))
 
-        sl_sb = load_rows(nc.gpsimd, "sl_sb", sl)
-        th_sb = load_rows(nc.gpsimd, "th_sb", th)
-        n2_sb = load_list("n2_sb", n2)
+        sl_sb = load_rows(nc.sync, "sl_sb", sl)
+        th_sb = load_rows(nc.sync, "th_sb", th)
         n1_sb = load_list("n1_sb", n1)
-        w3w_raw = load_words("w3w_raw", w3_words, N)
         load_scale_rows(nc.sync, raw_planes[2], 0, w3_scales)
         tau_sb = load_rows(nc.sync, "tau_sb", tau)
         n3_sb = load_list("n3_sb", n3)
@@ -119,17 +121,18 @@ def tile_picked_twhgxbelg_none_po_kernel(
 
         offs_plane = sb("offs_plane", [P, S], U8)
         nc.vector.tensor_copy(offs_plane[:], xs_table[:].indirect(offs_sb[:]))
-        offs_words = sb("offs_words", [P, S], U32)
-        nc.vector.tensor_copy(offs_words[:], xw_table[:].indirect(offs_sb[:]))
+        w1s = deal(nc.gpsimd.tensor_copy, "w1s", raw_planes[0], U8)
+        offs_words = {}
+        for first in (0, HALF):
+            offs_words[first] = sb(f"offs_words{first}", [P, HALF], U32)
+            nc.vector.tensor_copy(offs_words[first][:], xw_table[:].indirect(entries(offs_sb, first, HALF)))
         hz_words = sb("hz_words", [P, S], U32)
         nc.vector.tensor_copy(hz_words[:], xw_table[:].indirect(hz_sb[:]))
+        w2s = deal(nc.gpsimd.tensor_copy, "w2s", raw_planes[1], U8)
 
         w1w = deal(nc.scalar.copy, "w1w", w1w_raw, U32)
+        w3w = deal(nc.scalar.copy, "w3w", w3w_raw, U32)
         w2w = deal(nc.scalar.copy, "w2w", w2w_raw, U32)
-        w1s = deal(nc.gpsimd.tensor_copy, "w1s", raw_planes[0], U8)
-        w2s = deal(nc.gpsimd.tensor_copy, "w2s", raw_planes[1], U8)
-        w3w = deal(nc.gpsimd.tensor_copy, "w3w", w3w_raw, U32)
-        w3s = deal(nc.gpsimd.tensor_copy, "w3s", raw_planes[2], U8)
 
         half_gn = sb("half_gn", [P, PACK], F32)
         nc.gpsimd.tensor_scalar(half_gn[:], gn_sb[:], -0.5, 0.0, ALU.mult, ALU.add)
@@ -137,6 +140,8 @@ def tile_picked_twhgxbelg_none_po_kernel(
         nc.gpsimd.tensor_scalar(minus_sl[:], sl_sb[:], -1.0, 0.0, ALU.mult, ALU.add)
         sg_bias = sb("sg_bias", [P, PACK], F32)
         nc.gpsimd.tensor_tensor(sg_bias[:], minus_sl[:], th_sb[:], ALU.mult)
+
+        w3s = deal(nc.gpsimd.tensor_copy, "w3s", raw_planes[2], U8)
 
         d_ps = [psum.tile([P, S], F32, name=f"d_ps{t}", tag=f"bank{t}") for t in range(PACK)]
         y_ps = [psum.tile([P, S], F32, name=f"y_ps{t}", tag=f"bank{PACK + t}") for t in range(PACK)]
@@ -149,14 +154,15 @@ def tile_picked_twhgxbelg_none_po_kernel(
             )
 
         for t in range(PACK):
-            product(y_ps[t][:], w1w, w1s, t, offs_words[:], offs_plane[:])
+            for first in (0, HALF):
+                half = slice(first, first + HALF)
+                product(y_ps[t][:, half], w1w, w1s[:], t, offs_words[first][:], offs_plane[:, half])
         for t in range(PACK):
-            product(d_ps[t][:], w2w, w2s, t, hz_words[:], hz_plane[:])
+            product(d_ps[t][:], w2w, w2s[:], t, hz_words[:], hz_plane[:])
 
         d_sb = [sb(f"d_sb{t}", [P, S], F32) for t in range(PACK)]
         y_sb = [sb(f"y_sb{t}", [P, S], F32) for t in range(PACK)]
         h_sg = [sb(f"h_sg{t}", [P, 2 * S], F32) for t in range(PACK)]
-        near = sb("near", [P, PACK, S], F32)
         gated = sb("gated", [P, PACK, S], F32)
         z_bf = sb("z_bf", [P, PACK * S], BF16)
         z_words = sb("z_words", [P, S], U32)
@@ -165,55 +171,61 @@ def tile_picked_twhgxbelg_none_po_kernel(
         ea_bias = sb("ea_bias", [P, PACK], F32)
         h_ps = []
 
-        def h_out(t, c):
+        def h_out(t, step):
+            c = step if t < 2 else PACK - 1 - step
             nc.vector.tensor_scalar(
                 h_sg[t][:, c * BANK_COLS : (c + 1) * BANK_COLS], h_ps[c][:, t, :], 1.0,
-                tops[:, t, c - 1 : c] if c else None, ALU.mult, ALU.max, accum_out=tops[:, t, c : c + 1],
+                tops[:, t, step - 1 : step] if step else None, ALU.mult, ALU.max, accum_out=tops[:, t, step : step + 1],
             )
+
+        def fetch_near(gather, first, count, tag):
+            near = sb(f"near{first}", [P, PACK, count], F32, tag=tag)
+            for t in range(PACK):
+                gather(near[:, t, :], y_sb[t][:].indirect(entries(n2_sb, first, count)))
+            return near
+
+        def scalar_gather(out, window):
+            nc.scalar.activation(out, window, ACT.Copy)
+
+        def gate(t, first):
+            half = slice(first, first + HALF)
+            sg = h_sg[t][:, S + first : S + first + HALF]
+            nc.scalar.activation(
+                sg, d_sb[t][:].indirect(entries(n1_sb, first, HALF)), ACT.Sigmoid,
+                bias=sg_bias[:, t : t + 1], scale=sl_sb[:, t : t + 1],
+            )
+            nc.vector.scalar_tensor_tensor(
+                gated[:, t, half], y_ps[t][:, half], gn_sb[:, t : t + 1], sg, ALU.mult, ALU.mult
+            )
+
+        def third_product(first, count, near):
+            cols = slice(first, first + count)
+            z_cols = z_bf[:, PACK * first : PACK * (first + count)]
+            nc.vector.tensor_tensor(interleaved(z_cols, count), paired(gated[:, :, cols]), paired(near[:]), ALU.add)
+            nc.vector.quantize_mx(out=z_words[:, cols].bitcast(FP8X4), scales=z_plane[:, cols], in_=z_cols)
+            for c in range(first // BANK_COLS, (first + count) // BANK_COLS):
+                bank = psum.tile([P, PACK, BANK_COLS], F32, name=f"h_ps{c}", tag=f"bank{c}")
+                h_ps.append(bank)
+                c_cols = slice(c * BANK_COLS, (c + 1) * BANK_COLS)
+                for t in range(PACK):
+                    product(bank[:, t, :], w3w, w3s[:], t, z_words[:, c_cols], z_plane[:, c_cols])
+                    if t == 0:
+                        h_out(0, c)
 
         for t in range(PACK):
             nc.scalar.activation(y_sb[t][:], y_ps[t][:], ACT.Copy, scale=half_gn[:, t : t + 1])
-        def fetch_near(t, first, on_scalar):
-            window = y_sb[t][:].indirect(entries(n2_sb, first, HALF))
-            if on_scalar:
-                nc.scalar.activation(near[:, t, first : first + HALF], window, ACT.Copy)
-            else:
-                nc.vector.tensor_copy(near[:, t, first : first + HALF], window)
-
+        near_a = fetch_near(nc.vector.tensor_copy, 0, HALF, None)
         for t in range(PACK):
-            fetch_near(t, 0, False)
-        for t in range(PACK - NEAR_ON_SCALAR):
-            fetch_near(t, HALF, False)
-
-        for first, z_chunks in Z_CHUNKS:
-            half = slice(first, first + HALF)
-            for t in range(PACK):
-                if first == 0:
-                    nc.scalar.copy(d_sb[t][:], d_ps[t][:])
-                sg = h_sg[t][:, S + first : S + first + HALF]
-                nc.scalar.activation(
-                    sg, d_sb[t][:].indirect(entries(n1_sb, first, HALF)), ACT.Sigmoid,
-                    bias=sg_bias[:, t : t + 1], scale=sl_sb[:, t : t + 1],
-                )
-                nc.vector.scalar_tensor_tensor(
-                    gated[:, t, half], y_ps[t][:, half], gn_sb[:, t : t + 1], sg, ALU.mult, ALU.mult
-                )
-            if first:
-                for t in range(PACK - NEAR_ON_SCALAR, PACK):
-                    fetch_near(t, HALF, True)
-            for count in z_chunks:
-                cols = slice(first, first + count)
-                z_cols = z_bf[:, PACK * first : PACK * (first + count)]
-                nc.vector.tensor_tensor(interleaved(z_cols, count), paired(gated[:, :, cols]), paired(near[:, :, cols]), ALU.add)
-                nc.vector.quantize_mx(out=z_words[:, cols].bitcast(FP8X4), scales=z_plane[:, cols], in_=z_cols)
-                for c in range(first // BANK_COLS, (first + count) // BANK_COLS):
-                    bank = psum.tile([P, PACK, BANK_COLS], F32, name=f"h_ps{c}", tag=f"bank{c}")
-                    h_ps.append(bank)
-                    c_cols = slice(c * BANK_COLS, (c + 1) * BANK_COLS)
-                    for t in range(PACK):
-                        product(bank[:, t, :], w3w, w3s, t, z_words[:, c_cols], z_plane[:, c_cols])
-                    h_out(0, c)
-                first = first + count
+            d_copy = nc.vector.tensor_copy if t else nc.scalar.copy
+            d_copy(d_sb[t][:], d_ps[t][:])
+            gate(t, 0)
+        third_product(0, HALF, near_a)
+        for t in range(PACK):
+            gate(t, HALF)
+        near_b = fetch_near(scalar_gather, HALF, BANK_COLS, "d_sb2")
+        near_c = fetch_near(scalar_gather, HALF + BANK_COLS, BANK_COLS, "d_sb3")
+        third_product(HALF, BANK_COLS, near_b)
+        third_product(HALF + BANK_COLS, BANK_COLS, near_c)
 
         total = sb("total", [P, PACK, S], F32)
         for t in range(PACK):
@@ -244,11 +256,14 @@ def tile_picked_twhgxbelg_none_po_kernel(
             nc.vector.tensor_tensor(res[:], logs[:], h_ps[c][:], ALU.add)
             nc.sync.dma_start(out_rows[:, :, cols], res[:])
             results.append(res)
-        round_copies = (nc.scalar.copy, nc.scalar.copy, nc.vector.tensor_copy, nc.vector.tensor_copy)
+        round_copies = (None, nc.scalar.copy, nc.scalar.copy, nc.vector.tensor_copy)
         for c in range(PACK):
             cols = slice(c * BANK_COLS, (c + 1) * BANK_COLS)
             res_bf = sb(f"res_bf{c}", [P, PACK * BANK_COLS], BF16)
-            round_copies[c](interleaved(res_bf[:], BANK_COLS), paired(results[c][:]))
+            if c:
+                round_copies[c](interleaved(res_bf[:], BANK_COLS), paired(results[c][:]))
+            else:
+                nc.gpsimd.tensor_copy(res_bf[:].rearrange("p (c t) -> p c t", t=PACK), results[c][:].rearrange("p t c -> p c t"))
             nc.vector.quantize_mx(out=o_words[:, cols].bitcast(FP8X4), scales=o_plane[:, cols], in_=res_bf[:])
             if c % 2:
                 pair = slice((c - 1) * BANK_COLS, (c + 1) * BANK_COLS)

@@ -17,17 +17,32 @@ ACT = mybir.ActivationFunctionType
 
 P = 128
 PACK = 4
+QUAD = 32
 LANES = 16
-BANK_COLS = 128
+LINE = 16
 HALF = S // 2
+BANK_COLS = S // PACK
+LAST = PACK - 1
 
 
 def words_of(dram):
     return dram[0].rearrange("p n t -> p (n t)").bitcast(I32)
 
 
+def rows_by_place(dram):
+    return dram[0].bitcast(I32).rearrange("(q i) c -> i q c", i=PACK)
+
+
 def entries(offsets, first, count):
     return offsets[:, first // LANES : (first + count) // LANES]
+
+
+def interleaved(ap):
+    return ap.rearrange("p (c i t) -> p c t i", i=2, t=PACK)
+
+
+def paired(ap):
+    return ap.rearrange("p t (c i) -> p c t i", i=2)
 
 
 def tile_picked_twhgxbelg_none_po_kernel(
@@ -47,109 +62,106 @@ def tile_picked_twhgxbelg_none_po_kernel(
             nc.sync.dma_start(tile[:], dram)
             return tile
 
-        def load_rows(queue, name, dram):
+        def load_words(name, dram, width):
+            tile = sb(name, [P, width], U32)
+            nc.sync.dma_start(tile[:].bitcast(I32), words_of(dram))
+            return tile
+
+        def load_column(queue, name, dram):
             tile = sb(name, [P, PACK], F32)
             queue.dma_start(tile[:], dram.rearrange("(p t) o -> p (t o)", t=PACK))
             return tile
 
-        def load_scale_rows(queue, tile, first, dram):
-            rows = dram[0].bitcast(I32).rearrange("(q i) c -> i q c", i=4)
-            for i in range(4):
-                queue.dma_start(tile[first + i : P : 32, :].bitcast(I32), rows[i])
+        def load_plane(tile, dram):
+            for i in range(PACK):
+                nc.sync.dma_start(tile[i:P:QUAD, :].bitcast(I32), rows_by_place(dram)[i])
 
-        def deal(engine_copy, name, raw, dtype, tag=None):
-            dealt = sb(name, [P, H], dtype, tag=tag)
-            run = 16 if dtype == U8 else 4
+        def deal(engine_copy, name, raw, dtype, run):
+            dealt = sb(name, [P, H], dtype)
             engine_copy(
                 dealt[:].rearrange("p (t g i) -> p g t i", t=PACK, i=run),
                 raw[:].rearrange("p (g i t) -> p g t i", t=PACK, i=run),
             )
             return dealt
 
-        def interleaved(tile, width):
-            return tile.rearrange("p (c i t) -> p c t i", i=2, t=PACK)
+        def deal_words(name, raw):
+            return deal(nc.scalar.copy, name, raw, U32, LINE // 4)
 
-        def paired(tile):
-            return tile.rearrange("p t (c i) -> p c t i", i=2)
+        def deal_bytes(name, raw):
+            return deal(nc.gpsimd.tensor_copy, name, raw, U8, LINE)
 
         xs_table = sb("xs_table", [P, T], U8)
         raw_planes = [sb(f"w{i}s_raw", [P, H], U8) for i in (1, 2, 3)]
         for tile in [xs_table] + raw_planes:
             nc.vector.memset(tile[:].bitcast(I32), 0)
+
         warm_in = sb("warm_in", [P, 1], F32)
         nc.vector.memset(warm_in[:], 0.0)
         warm_out = sb("warm_out", [P, 1], F32)
         nc.scalar.activation(warm_out[:], warm_in[:], ACT.Sigmoid)
 
-        def load_words(name, dram, width):
-            tile = sb(name, [P, width], U32)
-            nc.sync.dma_start(tile[:].bitcast(I32), words_of(dram))
-            return tile
-
         w1w_raw = load_words("w1w_raw", w1_words, H)
         hz_sb = load_list("hz_sb", hz)
-        xs_rows = x_scales[0].bitcast(I32)
-        by_run = xs_rows.rearrange("(r e) c -> e r c", e=2)
-        by_quad = xs_rows.rearrange("(q i) c -> i q c", i=4)
+        rows_by_run = x_scales[0].bitcast(I32).rearrange("(r e) c -> e r c", e=2)
         for e in range(2):
-            nc.sync.dma_start(xs_table[e:P:LANES, :].bitcast(I32), by_run[e])
+            nc.sync.dma_start(xs_table[e:P:LANES, :].bitcast(I32), rows_by_run[e])
         for i in (2, 3):
-            nc.sync.dma_start(xs_table[i:P:32, :].bitcast(I32), by_quad[i])
+            nc.sync.dma_start(xs_table[i:P:QUAD, :].bitcast(I32), rows_by_place(x_scales)[i])
         offs_sb = load_list("offs_sb", offs)
         xw_table = load_words("xw_table", x_words, T)
-        load_scale_rows(nc.sync, raw_planes[0], 0, w1_scales)
+        load_plane(raw_planes[0], w1_scales)
         w3w_raw = load_words("w3w_raw", w3_words, N)
-        gn_sb = load_rows(nc.gpsimd, "gn_sb", gn)
+        gn_sb = load_column(nc.gpsimd, "gn_sb", gn)
         w2w_raw = load_words("w2w_raw", w2_words, H)
         n2_sb = load_list("n2_sb", n2)
-        load_scale_rows(nc.sync, raw_planes[1], 0, w2_scales)
+        load_plane(raw_planes[1], w2_scales)
 
         hz_bytes = sb("hz_bytes", [P, S], U8)
         nc.vector.tensor_copy(hz_bytes[:], xs_table[:].indirect(hz_sb[:]))
         hz_plane = sb("hz_plane", [P, S], U8)
         nc.vector.tensor_copy(hz_plane[:].bitcast(I32), hz_bytes[:].bitcast(I32))
         for e in range(2):
-            nc.sync.dma_start(hz_plane[2 + e : P : 32, :].bitcast(I32), hz_bytes[LANES + e : P : 32, :].bitcast(I32))
+            nc.sync.dma_start(hz_plane[2 + e : P : QUAD, :].bitcast(I32), hz_bytes[LANES + e : P : QUAD, :].bitcast(I32))
 
-        sl_sb = load_rows(nc.sync, "sl_sb", sl)
-        th_sb = load_rows(nc.sync, "th_sb", th)
+        sl_sb = load_column(nc.sync, "sl_sb", sl)
+        th_sb = load_column(nc.sync, "th_sb", th)
         n1_sb = load_list("n1_sb", n1)
-        load_scale_rows(nc.sync, raw_planes[2], 0, w3_scales)
-        tau_sb = load_rows(nc.sync, "tau_sb", tau)
+        load_plane(raw_planes[2], w3_scales)
+        tau_sb = load_column(nc.sync, "tau_sb", tau)
         n3_sb = load_list("n3_sb", n3)
         n4_sb = load_list("n4_sb", n4)
 
         offs_plane = sb("offs_plane", [P, S], U8)
         nc.vector.tensor_copy(offs_plane[:], xs_table[:].indirect(offs_sb[:]))
-        w1s = deal(nc.gpsimd.tensor_copy, "w1s", raw_planes[0], U8)
+        w1s = deal_bytes("w1s", raw_planes[0])
         offs_words = {}
         for first in (0, HALF):
             offs_words[first] = sb(f"offs_words{first}", [P, HALF], U32)
             nc.vector.tensor_copy(offs_words[first][:], xw_table[:].indirect(entries(offs_sb, first, HALF)))
         hz_words = sb("hz_words", [P, S], U32)
         nc.vector.tensor_copy(hz_words[:], xw_table[:].indirect(hz_sb[:]))
-        w2s = deal(nc.gpsimd.tensor_copy, "w2s", raw_planes[1], U8)
+        w2s = deal_bytes("w2s", raw_planes[1])
 
-        w1w = deal(nc.scalar.copy, "w1w", w1w_raw, U32)
-        w3w = deal(nc.scalar.copy, "w3w", w3w_raw, U32)
-        w2w = deal(nc.scalar.copy, "w2w", w2w_raw, U32)
+        w1w = deal_words("w1w", w1w_raw)
+        w3w = deal_words("w3w", w3w_raw)
+        w2w = deal_words("w2w", w2w_raw)
 
-        half_gn = sb("half_gn", [P, PACK], F32)
-        nc.gpsimd.tensor_scalar(half_gn[:], gn_sb[:], -0.5, 0.0, ALU.mult, ALU.add)
+        minus_half_gn = sb("half_gn", [P, PACK], F32)
+        nc.gpsimd.tensor_scalar(minus_half_gn[:], gn_sb[:], -0.5, 0.0, ALU.mult, ALU.add)
         minus_sl = sb("minus_sl", [P, PACK], F32)
         nc.gpsimd.tensor_scalar(minus_sl[:], sl_sb[:], -1.0, 0.0, ALU.mult, ALU.add)
         sg_bias = sb("sg_bias", [P, PACK], F32)
         nc.gpsimd.tensor_tensor(sg_bias[:], minus_sl[:], th_sb[:], ALU.mult)
 
-        w3s = deal(nc.gpsimd.tensor_copy, "w3s", raw_planes[2], U8)
+        w3s = deal_bytes("w3s", raw_planes[2])
 
         d_ps = [psum.tile([P, S], F32, name=f"d_ps{t}", tag=f"bank{t}") for t in range(PACK)]
         y_ps = [psum.tile([P, S], F32, name=f"y_ps{t}", tag=f"bank{PACK + t}") for t in range(PACK)]
 
         def product(out, w, w_plane, t, x, x_plane):
-            cols = slice(t * P, (t + 1) * P)
+            w_cols = slice(t * P, (t + 1) * P)
             nc.tensor.matmul_mx(
-                out=out, lhsT=w[:, cols].bitcast(FP8X4), lhsT_scale=w_plane[:, cols],
+                out=out, lhsT=w[:, w_cols].bitcast(FP8X4), lhsT_scale=w_plane[:, w_cols],
                 rhs=x.bitcast(FP8X4), rhs_scale=x_plane, start=True, stop=True,
             )
 
@@ -168,11 +180,11 @@ def tile_picked_twhgxbelg_none_po_kernel(
         z_words = sb("z_words", [P, S], U32)
         z_plane = sb("z_plane", [P, S], U8)
         tops = sb("tops", [P, PACK, PACK], F32)
-        ea_bias = sb("ea_bias", [P, PACK], F32)
+        exp_bias = sb("ea_bias", [P, PACK], F32)
         h_ps = []
 
         def h_out(t, step):
-            c = step if t < 2 else PACK - 1 - step
+            c = step if t < 2 else LAST - step
             nc.vector.tensor_scalar(
                 h_sg[t][:, c * BANK_COLS : (c + 1) * BANK_COLS], h_ps[c][:, t, :], 1.0,
                 tops[:, t, step - 1 : step] if step else None, ALU.mult, ALU.max, accum_out=tops[:, t, step : step + 1],
@@ -201,22 +213,23 @@ def tile_picked_twhgxbelg_none_po_kernel(
         def third_product(first, count, near):
             cols = slice(first, first + count)
             z_cols = z_bf[:, PACK * first : PACK * (first + count)]
-            nc.vector.tensor_tensor(interleaved(z_cols, count), paired(gated[:, :, cols]), paired(near[:]), ALU.add)
+            nc.vector.tensor_tensor(interleaved(z_cols), paired(gated[:, :, cols]), paired(near[:]), ALU.add)
             nc.vector.quantize_mx(out=z_words[:, cols].bitcast(FP8X4), scales=z_plane[:, cols], in_=z_cols)
             for c in range(first // BANK_COLS, (first + count) // BANK_COLS):
                 bank = psum.tile([P, PACK, BANK_COLS], F32, name=f"h_ps{c}", tag=f"bank{c}")
                 h_ps.append(bank)
-                c_cols = slice(c * BANK_COLS, (c + 1) * BANK_COLS)
+                bank_cols = slice(c * BANK_COLS, (c + 1) * BANK_COLS)
+                read_after = 0 if c == LAST else LAST
                 for t in range(PACK):
-                    product(bank[:, t, :], w3w, w3s[:], t, z_words[:, c_cols], z_plane[:, c_cols])
-                    if t == 0:
+                    product(bank[:, t, :], w3w, w3s[:], t, z_words[:, bank_cols], z_plane[:, bank_cols])
+                    if t == read_after:
                         h_out(0, c)
 
         for t in range(PACK):
-            nc.scalar.activation(y_sb[t][:], y_ps[t][:], ACT.Copy, scale=half_gn[:, t : t + 1])
+            nc.scalar.activation(y_sb[t][:], y_ps[t][:], ACT.Copy, scale=minus_half_gn[:, t : t + 1])
         near_a = fetch_near(nc.vector.tensor_copy, 0, HALF, None)
         for t in range(PACK):
-            d_copy = nc.vector.tensor_copy if t else nc.scalar.copy
+            d_copy = nc.scalar.copy if t < 2 else nc.vector.tensor_copy
             d_copy(d_sb[t][:], d_ps[t][:])
             gate(t, 0)
         third_product(0, HALF, near_a)
@@ -228,21 +241,29 @@ def tile_picked_twhgxbelg_none_po_kernel(
         third_product(HALF + BANK_COLS, BANK_COLS, near_c)
 
         total = sb("total", [P, PACK, S], F32)
-        for t in range(PACK):
-            if t:
-                for c in range(PACK):
-                    h_out(t, c)
+
+        def make_bias(t):
             nc.vector.scalar_tensor_tensor(
-                ea_bias[:, t : t + 1], tops[:, t, PACK - 1 : PACK], -1.0, tau_sb[:, t : t + 1], ALU.mult, ALU.mult
+                exp_bias[:, t : t + 1], tops[:, t, LAST:PACK], -1.0, tau_sb[:, t : t + 1], ALU.mult, ALU.mult
             )
-            both = []
-            for name, lst in (("ea", n3_sb), ("eb", n4_sb)):
-                e = sb(f"{name}{t}", [P, S], F32)
+
+        make_bias(0)
+        for tiles in ((1,), (2, 3)):
+            for step in range(PACK):
+                for t in tiles:
+                    h_out(t, step)
+            for t in tiles:
+                make_bias(t)
+        for t in range(PACK):
+            exps = []
+            for name, offsets in (("ea", n3_sb), ("eb", n4_sb)):
+                fetched = sb(f"{name}{t}", [P, S], F32)
                 nc.scalar.activation(
-                    e[:], h_sg[t][:].indirect(lst[:]), ACT.Exp, bias=ea_bias[:, t : t + 1], scale=tau_sb[:, t : t + 1]
+                    fetched[:], h_sg[t][:].indirect(offsets[:]), ACT.Exp,
+                    bias=exp_bias[:, t : t + 1], scale=tau_sb[:, t : t + 1],
                 )
-                both.append(e)
-            nc.vector.scalar_tensor_tensor(total[:, t, :], both[0][:], 0.25, both[1][:], ALU.add, ALU.add)
+                exps.append(fetched)
+            nc.vector.scalar_tensor_tensor(total[:, t, :], exps[0][:], 0.25, exps[1][:], ALU.add, ALU.add)
 
         out_rows = out_0.rearrange("(p t) c -> p t c", t=PACK)
         o_words = sb("o_words", [P, S], U32)
@@ -256,19 +277,19 @@ def tile_picked_twhgxbelg_none_po_kernel(
             nc.vector.tensor_tensor(res[:], logs[:], h_ps[c][:], ALU.add)
             nc.sync.dma_start(out_rows[:, :, cols], res[:])
             results.append(res)
-        round_copies = (None, nc.scalar.copy, nc.scalar.copy, nc.vector.tensor_copy)
+
         for c in range(PACK):
             cols = slice(c * BANK_COLS, (c + 1) * BANK_COLS)
             res_bf = sb(f"res_bf{c}", [P, PACK * BANK_COLS], BF16)
-            if c:
-                round_copies[c](interleaved(res_bf[:], BANK_COLS), paired(results[c][:]))
-            else:
+            if c == 0:
                 nc.gpsimd.tensor_copy(res_bf[:].rearrange("p (c t) -> p c t", t=PACK), results[c][:].rearrange("p t c -> p c t"))
+            else:
+                round_copy = nc.vector.tensor_copy if c == LAST else nc.scalar.copy
+                round_copy(interleaved(res_bf[:]), paired(results[c][:]))
             nc.vector.quantize_mx(out=o_words[:, cols].bitcast(FP8X4), scales=o_plane[:, cols], in_=res_bf[:])
             if c % 2:
                 pair = slice((c - 1) * BANK_COLS, (c + 1) * BANK_COLS)
                 nc.sync.dma_start(words_of(out_1)[:, pair], o_words[:, pair].bitcast(I32))
-        plane_rows = out_2[0].bitcast(I32).rearrange("(q i) c -> i q c", i=4)
-        for i in range(4):
+        for i in range(PACK):
             queue = nc.scalar if i % 2 else nc.sync
-            queue.dma_start(plane_rows[i], o_plane[i:P:32, :].bitcast(I32))
+            queue.dma_start(rows_by_place(out_2)[i], o_plane[i:P:QUAD, :].bitcast(I32))

from contextlib import ExitStack

import concourse.mybir as mybir

K, T, S, N, H = 512, 2048, 512, 512, 512
FLOPS = 2 * K * H * S * 2 + 2 * H * N * S

F32 = mybir.dt.float32
BF16 = mybir.dt.bfloat16
I32 = mybir.dt.int32
U32 = mybir.dt.uint32
U16 = mybir.dt.uint16
U8 = mybir.dt.uint8
FP8X4 = mybir.dt.float8_e4m3fn_x4
ALU = mybir.AluOpType
ACT = mybir.ActivationFunctionType

P = 128
PACK = 4
QUAD = 32
LANES = 16
LINE = 16
HALF = S // 2
BANK_COLS = S // PACK
LAST = PACK - 1


def words_of(dram):
    return dram[0].rearrange("p n t -> p (n t)").bitcast(I32)


def rows_by_place(dram):
    return dram[0].bitcast(I32).rearrange("(q i) c -> i q c", i=PACK)


def entries(offsets, first, count):
    return offsets[:, first // LANES : (first + count) // LANES]


def interleaved(ap):
    return ap.rearrange("p (c i t) -> p c t i", i=2, t=PACK)


def paired(ap):
    return ap.rearrange("p t (c i) -> p c t i", i=2)


def tile_picked_twhgxbelg_none_po_kernel(
    tc, x_words, x_scales, w1_words, w1_scales, w2_words, w2_scales, sl, th, gn,
    w3_words, w3_scales, tau, offs, hz, n1, n2, n3, n4, out_0, out_1, out_2,
):
    nc = tc.nc
    with ExitStack() as ctx:
        keep = ctx.enter_context(tc.tile_pool(name="keep", bufs=1))
        psum = ctx.enter_context(tc.psum_pool(name="psum", bufs=1))

        def sb(name, shape, dtype, tag=None):
            return keep.tile(shape, dtype, name=name, tag=tag or name, align_bytes=64)

        def load_list(name, dram):
            tile = sb(name, [P, S // LANES], U16)
            nc.sync.dma_start(tile[:], dram)
            return tile

        def load_words(name, dram, width):
            tile = sb(name, [P, width], U32)
            nc.sync.dma_start(tile[:].bitcast(I32), words_of(dram))
            return tile

        def load_column(queue, name, dram):
            tile = sb(name, [P, PACK], F32)
            queue.dma_start(tile[:], dram.rearrange("(p t) o -> p (t o)", t=PACK))
            return tile

        def load_plane(tile, dram):
            for i in range(PACK):
                nc.sync.dma_start(tile[i:P:QUAD, :].bitcast(I32), rows_by_place(dram)[i])

        def deal(engine_copy, name, raw, dtype, run):
            dealt = sb(name, [P, H], dtype)
            engine_copy(
                dealt[:].rearrange("p (t g i) -> p g t i", t=PACK, i=run),
                raw[:].rearrange("p (g i t) -> p g t i", t=PACK, i=run),
            )
            return dealt

        def deal_words(name, raw):
            return deal(nc.scalar.copy, name, raw, U32, LINE // 4)

        def deal_bytes(name, raw):
            return deal(nc.gpsimd.tensor_copy, name, raw, U8, LINE)

        xs_table = sb("xs_table", [P, T], U8)
        raw_planes = [sb(f"w{i}s_raw", [P, H], U8) for i in (1, 2, 3)]
        for tile in [xs_table] + raw_planes:
            nc.vector.memset(tile[:].bitcast(I32), 0)

        warm_in = sb("warm_in", [P, 1], F32)
        nc.vector.memset(warm_in[:], 0.0)
        warm_out = sb("warm_out", [P, 1], F32)
        nc.scalar.activation(warm_out[:], warm_in[:], ACT.Sigmoid)

        w1w_raw = load_words("w1w_raw", w1_words, H)
        hz_sb = load_list("hz_sb", hz)
        rows_by_run = x_scales[0].bitcast(I32).rearrange("(r e) c -> e r c", e=2)
        for e in range(2):
            nc.sync.dma_start(xs_table[e:P:LANES, :].bitcast(I32), rows_by_run[e])
        for i in (2, 3):
            nc.sync.dma_start(xs_table[i:P:QUAD, :].bitcast(I32), rows_by_place(x_scales)[i])
        offs_sb = load_list("offs_sb", offs)
        xw_table = load_words("xw_table", x_words, T)
        load_plane(raw_planes[0], w1_scales)
        w3w_raw = load_words("w3w_raw", w3_words, N)
        gn_sb = load_column(nc.gpsimd, "gn_sb", gn)
        w2w_raw = load_words("w2w_raw", w2_words, H)
        n2_sb = load_list("n2_sb", n2)
        load_plane(raw_planes[1], w2_scales)

        hz_bytes = sb("hz_bytes", [P, S], U8)
        nc.vector.tensor_copy(hz_bytes[:], xs_table[:].indirect(hz_sb[:]))
        hz_plane = sb("hz_plane", [P, S], U8)
        nc.vector.tensor_copy(hz_plane[:].bitcast(I32), hz_bytes[:].bitcast(I32))
        for e in range(2):
            nc.sync.dma_start(hz_plane[2 + e : P : QUAD, :].bitcast(I32), hz_bytes[LANES + e : P : QUAD, :].bitcast(I32))

        sl_sb = load_column(nc.sync, "sl_sb", sl)
        th_sb = load_column(nc.sync, "th_sb", th)
        n1_sb = load_list("n1_sb", n1)
        load_plane(raw_planes[2], w3_scales)
        tau_sb = load_column(nc.sync, "tau_sb", tau)
        n3_sb = load_list("n3_sb", n3)
        n4_sb = load_list("n4_sb", n4)

        offs_plane = sb("offs_plane", [P, S], U8)
        nc.vector.tensor_copy(offs_plane[:], xs_table[:].indirect(offs_sb[:]))
        w1s = deal_bytes("w1s", raw_planes[0])
        offs_words = {}
        for first in (0, HALF):
            offs_words[first] = sb(f"offs_words{first}", [P, HALF], U32)
            nc.vector.tensor_copy(offs_words[first][:], xw_table[:].indirect(entries(offs_sb, first, HALF)))
        hz_words = sb("hz_words", [P, S], U32)
        nc.vector.tensor_copy(hz_words[:], xw_table[:].indirect(hz_sb[:]))
        w2s = deal_bytes("w2s", raw_planes[1])

        w1w = deal_words("w1w", w1w_raw)
        w3w = deal_words("w3w", w3w_raw)
        w2w = deal_words("w2w", w2w_raw)

        minus_half_gn = sb("half_gn", [P, PACK], F32)
        nc.gpsimd.tensor_scalar(minus_half_gn[:], gn_sb[:], -0.5, 0.0, ALU.mult, ALU.add)
        minus_sl = sb("minus_sl", [P, PACK], F32)
        nc.gpsimd.tensor_scalar(minus_sl[:], sl_sb[:], -1.0, 0.0, ALU.mult, ALU.add)
        sg_bias = sb("sg_bias", [P, PACK], F32)
        nc.gpsimd.tensor_tensor(sg_bias[:], minus_sl[:], th_sb[:], ALU.mult)

        w3s = deal_bytes("w3s", raw_planes[2])

        d_ps = [psum.tile([P, S], F32, name=f"d_ps{t}", tag=f"bank{t}") for t in range(PACK)]
        y_ps = [psum.tile([P, S], F32, name=f"y_ps{t}", tag=f"bank{PACK + t}") for t in range(PACK)]

        def product(out, w, w_plane, t, x, x_plane):
            w_cols = slice(t * P, (t + 1) * P)
            nc.tensor.matmul_mx(
                out=out, lhsT=w[:, w_cols].bitcast(FP8X4), lhsT_scale=w_plane[:, w_cols],
                rhs=x.bitcast(FP8X4), rhs_scale=x_plane, start=True, stop=True,
            )

        for t in range(PACK):
            for first in (0, HALF):
                half = slice(first, first + HALF)
                product(y_ps[t][:, half], w1w, w1s[:], t, offs_words[first][:], offs_plane[:, half])
        for t in range(PACK):
            product(d_ps[t][:], w2w, w2s[:], t, hz_words[:], hz_plane[:])

        d_sb = [sb(f"d_sb{t}", [P, S], F32) for t in range(PACK)]
        y_sb = [sb(f"y_sb{t}", [P, S], F32) for t in range(PACK)]
        h_sg = [sb(f"h_sg{t}", [P, 2 * S], F32) for t in range(PACK)]
        gated = sb("gated", [P, PACK, S], F32)
        z_bf = sb("z_bf", [P, PACK * S], BF16)
        z_words = sb("z_words", [P, S], U32)
        z_plane = sb("z_plane", [P, S], U8)
        tops = sb("tops", [P, PACK, PACK], F32)
        exp_bias = sb("ea_bias", [P, PACK], F32)
        h_ps = []

        def h_out(t, step):
            c = step if t < 2 else LAST - step
            nc.vector.tensor_scalar(
                h_sg[t][:, c * BANK_COLS : (c + 1) * BANK_COLS], h_ps[c][:, t, :], 1.0,
                tops[:, t, step - 1 : step] if step else None, ALU.mult, ALU.max, accum_out=tops[:, t, step : step + 1],
            )

        def fetch_near(gather, first, count, tag):
            near = sb(f"near{first}", [P, PACK, count], F32, tag=tag)
            for t in range(PACK):
                gather(near[:, t, :], y_sb[t][:].indirect(entries(n2_sb, first, count)))
            return near

        def scalar_gather(out, window):
            nc.scalar.activation(out, window, ACT.Copy)

        def gate(t, first):
            half = slice(first, first + HALF)
            sg = h_sg[t][:, S + first : S + first + HALF]
            nc.scalar.activation(
                sg, d_sb[t][:].indirect(entries(n1_sb, first, HALF)), ACT.Sigmoid,
                bias=sg_bias[:, t : t + 1], scale=sl_sb[:, t : t + 1],
            )
            nc.vector.scalar_tensor_tensor(
                gated[:, t, half], y_ps[t][:, half], gn_sb[:, t : t + 1], sg, ALU.mult, ALU.mult
            )

        def third_product(first, count, near):
            cols = slice(first, first + count)
            z_cols = z_bf[:, PACK * first : PACK * (first + count)]
            nc.vector.tensor_tensor(interleaved(z_cols), paired(gated[:, :, cols]), paired(near[:]), ALU.add)
            nc.vector.quantize_mx(out=z_words[:, cols].bitcast(FP8X4), scales=z_plane[:, cols], in_=z_cols)
            for c in range(first // BANK_COLS, (first + count) // BANK_COLS):
                bank = psum.tile([P, PACK, BANK_COLS], F32, name=f"h_ps{c}", tag=f"bank{c}")
                h_ps.append(bank)
                bank_cols = slice(c * BANK_COLS, (c + 1) * BANK_COLS)
                read_after = 0 if c == LAST else LAST
                for t in range(PACK):
                    product(bank[:, t, :], w3w, w3s[:], t, z_words[:, bank_cols], z_plane[:, bank_cols])
                    if t == read_after:
                        h_out(0, c)

        for t in range(PACK):
            nc.scalar.activation(y_sb[t][:], y_ps[t][:], ACT.Copy, scale=minus_half_gn[:, t : t + 1])
        near_a = fetch_near(nc.vector.tensor_copy, 0, HALF, None)
        for t in range(PACK):
            d_copy = nc.scalar.copy if t < 2 else nc.vector.tensor_copy
            d_copy(d_sb[t][:], d_ps[t][:])
            gate(t, 0)
        third_product(0, HALF, near_a)
        for t in range(PACK):
            gate(t, HALF)
        near_b = fetch_near(scalar_gather, HALF, BANK_COLS, "d_sb2")
        near_c = fetch_near(scalar_gather, HALF + BANK_COLS, BANK_COLS, "d_sb3")
        third_product(HALF, BANK_COLS, near_b)
        third_product(HALF + BANK_COLS, BANK_COLS, near_c)

        total = sb("total", [P, PACK, S], F32)

        def make_bias(t):
            nc.vector.scalar_tensor_tensor(
                exp_bias[:, t : t + 1], tops[:, t, LAST:PACK], -1.0, tau_sb[:, t : t + 1], ALU.mult, ALU.mult
            )

        make_bias(0)
        for tiles in ((1,), (2, 3)):
            for step in range(PACK):
                for t in tiles:
                    h_out(t, step)
            for t in tiles:
                make_bias(t)
        for t in range(PACK):
            exps = []
            for name, offsets in (("ea", n3_sb), ("eb", n4_sb)):
                fetched = sb(f"{name}{t}", [P, S], F32)
                nc.scalar.activation(
                    fetched[:], h_sg[t][:].indirect(offsets[:]), ACT.Exp,
                    bias=exp_bias[:, t : t + 1], scale=tau_sb[:, t : t + 1],
                )
                exps.append(fetched)
            nc.vector.scalar_tensor_tensor(total[:, t, :], exps[0][:], 0.25, exps[1][:], ALU.add, ALU.add)

        out_rows = out_0.rearrange("(p t) c -> p t c", t=PACK)
        o_words = sb("o_words", [P, S], U32)
        o_plane = sb("o_plane", [P, S], U8)
        results = []
        for c in range(PACK):
            cols = slice(c * BANK_COLS, (c + 1) * BANK_COLS)
            logs = sb(f"logs{c}", [P, PACK, BANK_COLS], F32)
            nc.scalar.activation(logs[:], total[:, :, cols], ACT.Ln)
            res = sb(f"res{c}", [P, PACK, BANK_COLS], F32)
            nc.vector.tensor_tensor(res[:], logs[:], h_ps[c][:], ALU.add)
            nc.sync.dma_start(out_rows[:, :, cols], res[:])
            results.append(res)

        for c in range(PACK):
            cols = slice(c * BANK_COLS, (c + 1) * BANK_COLS)
            res_bf = sb(f"res_bf{c}", [P, PACK * BANK_COLS], BF16)
            if c == 0:
                nc.gpsimd.tensor_copy(res_bf[:].rearrange("p (c t) -> p c t", t=PACK), results[c][:].rearrange("p t c -> p c t"))
            else:
                round_copy = nc.vector.tensor_copy if c == LAST else nc.scalar.copy
                round_copy(interleaved(res_bf[:]), paired(results[c][:]))
            nc.vector.quantize_mx(out=o_words[:, cols].bitcast(FP8X4), scales=o_plane[:, cols], in_=res_bf[:])
            if c % 2:
                pair = slice((c - 1) * BANK_COLS, (c + 1) * BANK_COLS)
                nc.sync.dma_start(words_of(out_1)[:, pair], o_words[:, pair].bitcast(I32))
        for i in range(PACK):
            queue = nc.scalar if i % 2 else nc.sync
            queue.dma_start(rows_by_place(out_2)[i], o_plane[i:P:QUAD, :].bitcast(I32))
